import numpy as np
import ml_dtypes


def mxq(x, axis, fmt="e4m3"):
    dtype, down = {"e4m3": (ml_dtypes.float8_e4m3fn, 7), "e5m2": (ml_dtypes.float8_e5m2, 14)}[fmt]
    v = np.moveaxis(np.asarray(x, np.float32).astype(ml_dtypes.bfloat16).astype(np.float64), axis, -1)
    blocks = v.reshape(v.shape[:-1] + (-1, 32))
    amax = np.abs(blocks).max(-1, keepdims=True)
    byte = np.maximum(np.where(amax > 0, np.frexp(amax)[1] - 1 + 127, 0) - down, 1)
    scale = np.exp2(byte - 127.0)
    codes = (blocks / scale).astype(np.float32).astype(dtype).astype(np.float64)
    return np.moveaxis((codes * scale).reshape(v.shape), -1, axis)


WIDE = False


def mx_kscale(k):
    if not WIDE:
        return np.ones(k)
    levels = np.array([10, -10, 5, -5, 0])
    if k % 512:
        return np.exp2(np.random.permutation(np.resize(levels, k // 32))).repeat(32)
    a = np.empty((k // 512, 16))
    for p in range(k // 512):
        a[p, :8] = np.random.permutation(np.resize(levels, 8))
        for g in range(8):
            far = levels[np.abs(levels - a[p, g]) >= 10]
            a[p, g + 8] = far[np.random.randint(len(far))]
    return np.exp2(a.ravel()).repeat(32)


def f64(x):
    return np.asarray(x).astype(np.float64)


def striped(idx):
    return np.tile(np.asarray(idx).reshape(-1, 16).T, (8, 1)).astype(np.uint16)


def unstriped(offs):
    return offs[:16].T.reshape(-1).astype(np.int64)


E2M1 = np.array([0.0, 0.5, 1.0, 1.5, 2.0, 3.0, 4.0, 6.0, -0.0, -0.5, -1.0, -1.5, -2.0, -3.0, -4.0, -6.0])


def pack_weight(w, fmt):
    k, n = w.shape
    w = f64(np.asarray(w, np.float32).astype(ml_dtypes.bfloat16)).reshape(k // 32, 32, n)
    amax = np.abs(w).max(1)
    if fmt == "e4m3":
        byte = np.frexp(amax)[1] - 1 + 127 - 7
    else:
        mant, ex = np.frexp(amax / 6.0)
        byte = np.where(mant > 0.5, ex, ex - 1) + 127
    byte = np.clip(np.where(amax > 0, byte, 1), 1, 254)
    scaled = (w * np.exp2(127.0 - byte)[:, None, :]).reshape(k, n).astype(np.float32)
    by_word = np.ascontiguousarray(scaled.reshape(k // 512, 128, 4, n).transpose(0, 1, 3, 2))
    if fmt == "e4m3":
        words = by_word.astype(ml_dtypes.float8_e4m3fn).view(np.uint8)
    else:
        c = by_word.astype(ml_dtypes.float4_e2m1fn).view(np.uint8) & 0xF
        words = (c[..., 0::2] | (c[..., 1::2] << 4)).reshape(k // 512, 128, 2 * n)
    return np.ascontiguousarray(words), np.ascontiguousarray(byte.astype(np.uint8).reshape(k // 512, 16, n))


def unpack_weight(words, scales, fmt):
    g, _, n = scales.shape
    words = np.ascontiguousarray(words).reshape(g, 128, n, -1)
    if fmt == "e4m3":
        vals = words.view(ml_dtypes.float8_e4m3fn).astype(np.float64)
    else:
        nib = np.empty((g, 128, n, 4), np.uint8)
        nib[..., 0::2] = words & 0xF
        nib[..., 1::2] = words >> 4
        vals = E2M1[nib]
    vals = vals * np.repeat(np.exp2(scales.astype(np.float64) - 127.0), 8, axis=1)[..., None]
    return vals.transpose(0, 1, 3, 2).reshape(g * 512, n)


B, N, T, D, NQ = 2, 512, 2048, 512, 128


def setup_inputs():
    n = np.random.standard_normal
    jdx = np.random.permutation(1024)[:B * NQ]
    pages = np.random.permutation(T // 32)[:B * N // 32]
    idx = (pages[:, None] * 32 + np.arange(32)[None, :]).reshape(-1)
    s = mx_kscale(D)[:, None]
    kp = pack_weight(n((D, T)) / s, "e4m3")
    return {
        "qT": (n((D, 1024)) * s * (1.00 / np.sqrt(D))).astype(np.float32),
        "k_words": kp[0],
        "k_scales": kp[1],
        "offq": striped(jdx),
        "offs": striped(idx),
    }


def reference(qT, k_words, k_scales, offq, offs):
    jdx = unstriped(offq)
    idx = unstriped(offs)
    pick = lambda x, which: x[:, which].reshape(x.shape[0], B, -1).transpose(1, 0, 2)
    qg = mxq(pick(f64(qT), jdx), 1, "e4m3")
    k = unpack_weight(k_words, k_scales, "e4m3")
    kg = pick(k, idx)
    qq = qg
    a = qq.transpose(0, 2, 1) @ kg
    m = np.max(a, axis=-1, keepdims=True)
    e = np.exp(a - m)
    l = np.sum(e, axis=-1, keepdims=True)
    y = e / l
    return y

@@ -1,0 +1,111 @@
+from contextlib import ExitStack
+
+import concourse.mybir as mybir
+
+F32 = mybir.dt.float32
+BF16 = mybir.dt.bfloat16
+I32 = mybir.dt.int32
+U32 = mybir.dt.uint32
+U16 = mybir.dt.uint16
+U8 = mybir.dt.uint8
+FP8X4 = mybir.dt.float8_e4m3fn_x4
+ALU = mybir.AluOpType
+ACT = mybir.ActivationFunctionType
+AXIS = mybir.AxisListType
+
+P = 128
+PACK = 4
+B, N, T, D, NQ, QPOOL = 2, 512, 2048, 512, 128, 1024
+PIECE = 256
+FLOPS = 2 * B * NQ * N * D
+
+
+def tile_attend_lq_wts_kernel(tc, qT, k_words, k_scales, offq, offs, out):
+    nc = tc.nc
+    with ExitStack() as ctx:
+        lists = ctx.enter_context(tc.tile_pool(name="lists", bufs=1))
+        sb = ctx.enter_context(tc.tile_pool(name="sb", bufs=1))
+        psum = ctx.enter_context(tc.psum_pool(name="psum", bufs=1))
+
+        q_list = lists.tile([P, B * NQ // 16], U16, name="q_list")
+        k_list = lists.tile([P, B * N // 16], U16, name="k_list")
+        q_planes = [sb.tile([P, QPOOL], F32, name=f"q_plane{t}") for t in range(PACK)]
+        word_pool = sb.tile([P, T], I32, name="word_pool")
+        scale_pool = sb.tile([P, T // 4], I32, name="scale_pool")
+
+        q_rows = qT.rearrange("(p t) c -> p t c", t=PACK)
+        scale_rows = k_scales[0].bitcast(I32)
+
+        nc.vector.memset(scale_pool[:], 0)
+        warm_in = sb.tile([P, 8], F32, name="warm_in")
+        warm_out = sb.tile([P, 8], F32, name="warm_out")
+        nc.vector.memset(warm_in[:], 0.0)
+
+        nc.sync.dma_start(out=q_planes[0][:], in_=q_rows[:, 0, :])
+        nc.sync.dma_start(q_list[:], offq)
+        nc.sync.dma_start(k_list[:], offs)
+        for r in range(4):
+            nc.scalar.dma_start(out=scale_pool[r:P:32, :], in_=scale_rows[r:16:4, :])
+        for t in range(1, PACK):
+            nc.sync.dma_start(out=q_planes[t][:], in_=q_rows[:, t, :])
+        nc.sync.dma_start(out=word_pool[:], in_=k_words[0].rearrange("p n t -> p (n t)").bitcast(I32))
+        nc.scalar.activation(out=warm_out[:], in_=warm_in[:], func=ACT.Exp)
+
+        q_bf = sb.tile([P, B * NQ, PACK], BF16, name="q_bf", align_bytes=64)
+        q_codes = sb.tile([P, B * NQ], U32, name="q_codes", align_bytes=64)
+        q_scales = sb.tile([P, B * NQ], U8, name="q_scales", align_bytes=64)
+        k_codes = sb.tile([P, B * N], U32, name="k_codes", align_bytes=64)
+        k_sc = sb.tile([P, B * N], U8, name="k_sc", align_bytes=64)
+
+        def gather_plane(t):
+            nc.vector.tensor_copy(out=q_bf[:, :, t], in_=q_planes[t][:].indirect(q_list[:]))
+
+        def gather_scales(b):
+            nc.vector.tensor_copy(
+                out=k_sc[:, b * N:(b + 1) * N],
+                in_=scale_pool[:].bitcast(U8).indirect(k_list[:, b * N // 16:(b + 1) * N // 16]))
+
+        gather_plane(0)
+        gather_scales(0)
+        gather_plane(1)
+        gather_scales(1)
+        gather_plane(2)
+        gather_plane(3)
+        nc.vector.quantize_mx(out=q_codes[:].bitcast(FP8X4), scales=q_scales[:],
+                              in_=q_bf[:].rearrange("p c t -> p (c t)"))
+
+        scores = [psum.tile([P, N], F32, name=f"scores{b}") for b in range(B)]
+        for b in range(B):
+            qc = slice(b * NQ, (b + 1) * NQ)
+            for h in range(N // PIECE):
+                c0 = b * N + h * PIECE
+                kc = slice(c0, c0 + PIECE)
+                nc.vector.tensor_copy(
+                    out=k_codes[:, kc],
+                    in_=word_pool[:].bitcast(U32).indirect(k_list[:, c0 // 16:(c0 + PIECE) // 16]))
+                nc.tensor.matmul_mx(
+                    out=scores[b][:, h * PIECE:(h + 1) * PIECE],
+                    lhsT=q_codes[:, qc].bitcast(FP8X4), lhsT_scale=q_scales[:, qc],
+                    rhs=k_codes[:, kc].bitcast(FP8X4), rhs_scale=k_sc[:, kc],
+                    start=True, stop=True)
+
+        neg_max = [sb.tile([P, 1], F32, name=f"neg_max{b}") for b in range(B)]
+        row_sum = [sb.tile([P, 1], F32, name=f"row_sum{b}") for b in range(B)]
+        inv_sum = [sb.tile([P, 1], F32, name=f"inv_sum{b}") for b in range(B)]
+        expd = [sb.tile([P, N], F32, name=f"expd{b}") for b in range(B)]
+        res = [sb.tile([P, N], F32, name=f"res{b}") for b in range(B)]
+        for b in range(B):
+            nc.vector.tensor_reduce(out=neg_max[b][:], in_=scores[b][:], axis=AXIS.X, op=ALU.max, negate=True)
+        for b in range(B):
+            nc.scalar.activation(out=expd[b][:], in_=scores[b][:], func=ACT.Exp,
+                                 bias=neg_max[b][:], scale=1.0, accum_out=row_sum[b][:])
+        for b in range(B):
+            nc.vector.reciprocal(out=inv_sum[b][:], in_=row_sum[b][:])
+            for h in range(2):
+                cols = slice(h * N // 2, (h + 1) * N // 2)
+                nc.vector.tensor_scalar(out=res[b][:, cols], in0=expd[b][:, cols], scalar1=inv_sum[b][:],
+                                        scalar2=None, op0=ALU.mult)
+                queue = nc.sync if h == 0 else nc.scalar
+                if b == 0:
+                    queue = nc.sync
+                queue.dma_start(out=out[b, :, cols], in_=res[b][:, cols])

@@ -37,19 +37,16 @@ def tile_attend_lq_wts_kernel(tc, qT, k_words, k_scales, offq, offs, out):
         scale_rows = k_scales[0].bitcast(I32)
 
         nc.vector.memset(scale_pool[:], 0)
-        warm_in = sb.tile([P, 8], F32, name="warm_in")
-        warm_out = sb.tile([P, 8], F32, name="warm_out")
-        nc.vector.memset(warm_in[:], 0.0)
 
-        nc.sync.dma_start(out=q_planes[0][:], in_=q_rows[:, 0, :])
         nc.sync.dma_start(q_list[:], offq)
+        nc.sync.dma_start(out=q_planes[0][:], in_=q_rows[:, 0, :])
         nc.sync.dma_start(k_list[:], offs)
+        nc.sync.dma_start(out=q_planes[1][:], in_=q_rows[:, 1, :])
         for r in range(4):
-            nc.scalar.dma_start(out=scale_pool[r:P:32, :], in_=scale_rows[r:16:4, :])
-        for t in range(1, PACK):
+            nc.sync.dma_start(out=scale_pool[r:P:32, :], in_=scale_rows[r:16:4, :])
+        for t in range(2, PACK):
             nc.sync.dma_start(out=q_planes[t][:], in_=q_rows[:, t, :])
         nc.sync.dma_start(out=word_pool[:], in_=k_words[0].rearrange("p n t -> p (n t)").bitcast(I32))
-        nc.scalar.activation(out=warm_out[:], in_=warm_in[:], func=ACT.Exp)
 
         q_bf = sb.tile([P, B * NQ, PACK], BF16, name="q_bf", align_bytes=64)
         q_codes = sb.tile([P, B * NQ], U32, name="q_codes", align_bytes=64)
@@ -60,15 +57,11 @@ def tile_attend_lq_wts_kernel(tc, qT, k_words, k_scales, offq, offs, out):
         def gather_plane(t):
             nc.vector.tensor_copy(out=q_bf[:, :, t], in_=q_planes[t][:].indirect(q_list[:]))
 
-        def gather_scales(b):
-            nc.vector.tensor_copy(
-                out=k_sc[:, b * N:(b + 1) * N],
-                in_=scale_pool[:].bitcast(U8).indirect(k_list[:, b * N // 16:(b + 1) * N // 16]))
-
-        gather_plane(0)
-        gather_scales(0)
-        gather_plane(1)
-        gather_scales(1)
+        q_pair = sb.tile([P, 2, B * NQ], F32, name="q_pair")
+        for t in range(2):
+            nc.vector.tensor_copy(out=q_pair[:, t, :], in_=q_planes[t][:].indirect(q_list[:]))
+        nc.scalar.copy(out=q_bf[:, :, 0:2], in_=q_pair[:].rearrange("p t c -> p c t"))
+        nc.vector.tensor_copy(out=k_sc[:], in_=scale_pool[:].bitcast(U8).indirect(k_list[:]))
         gather_plane(2)
         gather_plane(3)
         nc.vector.quantize_mx(out=q_codes[:].bitcast(FP8X4), scales=q_scales[:],

@@ -41,10 +41,9 @@ def tile_attend_lq_wts_kernel(tc, qT, k_words, k_scales, offq, offs, out):
         nc.sync.dma_start(q_list[:], offq)
         nc.sync.dma_start(out=q_planes[0][:], in_=q_rows[:, 0, :])
         nc.sync.dma_start(k_list[:], offs)
-        nc.sync.dma_start(out=q_planes[1][:], in_=q_rows[:, 1, :])
         for r in range(4):
             nc.sync.dma_start(out=scale_pool[r:P:32, :], in_=scale_rows[r:16:4, :])
-        for t in range(2, PACK):
+        for t in range(1, PACK):
             nc.sync.dma_start(out=q_planes[t][:], in_=q_rows[:, t, :])
         nc.sync.dma_start(out=word_pool[:], in_=k_words[0].rearrange("p n t -> p (n t)").bitcast(I32))
 
@@ -57,10 +56,11 @@ def tile_attend_lq_wts_kernel(tc, qT, k_words, k_scales, offq, offs, out):
         def gather_plane(t):
             nc.vector.tensor_copy(out=q_bf[:, :, t], in_=q_planes[t][:].indirect(q_list[:]))
 
-        q_pair = sb.tile([P, 2, B * NQ], F32, name="q_pair")
+        q_cast = [sb.tile([P, QPOOL], BF16, name=f"q_cast{t}") for t in range(2)]
         for t in range(2):
-            nc.vector.tensor_copy(out=q_pair[:, t, :], in_=q_planes[t][:].indirect(q_list[:]))
-        nc.scalar.copy(out=q_bf[:, :, 0:2], in_=q_pair[:].rearrange("p t c -> p c t"))
+            nc.scalar.copy(out=q_cast[t][:], in_=q_planes[t][:])
+        for t in range(2):
+            nc.scalar.activation(out=q_bf[:, :, t], in_=q_cast[t][:].indirect(q_list[:]), func=ACT.Copy)
         nc.vector.tensor_copy(out=k_sc[:], in_=scale_pool[:].bitcast(U8).indirect(k_list[:]))
         gather_plane(2)
         gather_plane(3)

@@ -15,8 +15,17 @@ AXIS = mybir.AxisListType
 
 P = 128
 PACK = 4
+LIST_ROWS = 16
+QUADRANT = 32
+BLOCKS_PER_QUADRANT = 4
+BLOCK_PARTITIONS = 8
 B, N, T, D, NQ, QPOOL = 2, 512, 2048, 512, 128, 1024
-PIECE = 256
+
+KEY_PIECE = 256
+SCALAR_PLANES = (0, 1)
+VECTOR_PLANES = (2, 3)
+STORE_PIECE = N // 2
+
 FLOPS = 2 * B * NQ * N * D
 
 
@@ -27,78 +36,76 @@ def tile_attend_lq_wts_kernel(tc, qT, k_words, k_scales, offq, offs, out):
         sb = ctx.enter_context(tc.tile_pool(name="sb", bufs=1))
         psum = ctx.enter_context(tc.psum_pool(name="psum", bufs=1))
 
-        q_list = lists.tile([P, B * NQ // 16], U16, name="q_list")
-        k_list = lists.tile([P, B * N // 16], U16, name="k_list")
+        q_list = lists.tile([P, B * NQ // LIST_ROWS], U16, name="q_list")
+        k_list = lists.tile([P, B * N // LIST_ROWS], U16, name="k_list")
         q_planes = [sb.tile([P, QPOOL], F32, name=f"q_plane{t}") for t in range(PACK)]
         word_pool = sb.tile([P, T], I32, name="word_pool")
         scale_pool = sb.tile([P, T // 4], I32, name="scale_pool")
 
-        q_rows = qT.rearrange("(p t) c -> p t c", t=PACK)
-        scale_rows = k_scales[0].bitcast(I32)
-
         nc.vector.memset(scale_pool[:], 0)
 
-        nc.sync.dma_start(q_list[:], offq)
+        q_rows = qT.rearrange("(p t) c -> p t c", t=PACK)
         nc.sync.dma_start(out=q_planes[0][:], in_=q_rows[:, 0, :])
+        nc.sync.dma_start(q_list[:], offq)
         nc.sync.dma_start(k_list[:], offs)
-        for r in range(4):
-            nc.sync.dma_start(out=scale_pool[r:P:32, :], in_=scale_rows[r:16:4, :])
+        nc.sync.dma_start(out=scale_pool[0:P:BLOCK_PARTITIONS, :], in_=k_scales[0].bitcast(I32))
         for t in range(1, PACK):
             nc.sync.dma_start(out=q_planes[t][:], in_=q_rows[:, t, :])
         nc.sync.dma_start(out=word_pool[:], in_=k_words[0].rearrange("p n t -> p (n t)").bitcast(I32))
 
         q_bf = sb.tile([P, B * NQ, PACK], BF16, name="q_bf", align_bytes=64)
         q_codes = sb.tile([P, B * NQ], U32, name="q_codes", align_bytes=64)
-        q_scales = sb.tile([P, B * NQ], U8, name="q_scales", align_bytes=64)
+        q_scale_rows = sb.tile([P, B * NQ], U8, name="q_scale_rows", align_bytes=64)
         k_codes = sb.tile([P, B * N], U32, name="k_codes", align_bytes=64)
-        k_sc = sb.tile([P, B * N], U8, name="k_sc", align_bytes=64)
+        k_scale_picked = sb.tile([P, B * N], U8, name="k_scale_picked", align_bytes=64)
+        k_scale_words = sb.tile([P, B * N // 4], I32, name="k_scale_words", align_bytes=64)
+        k_scale_rows = k_scale_words[:].bitcast(U8)
 
-        def gather_plane(t):
-            nc.vector.tensor_copy(out=q_bf[:, :, t], in_=q_planes[t][:].indirect(q_list[:]))
-
-        q_cast = [sb.tile([P, QPOOL], BF16, name=f"q_cast{t}") for t in range(2)]
-        for t in range(2):
+        q_cast = [sb.tile([P, QPOOL], BF16, name=f"q_cast{t}") for t in SCALAR_PLANES]
+        for t in SCALAR_PLANES:
             nc.scalar.copy(out=q_cast[t][:], in_=q_planes[t][:])
-        for t in range(2):
+        for t in SCALAR_PLANES:
             nc.scalar.activation(out=q_bf[:, :, t], in_=q_cast[t][:].indirect(q_list[:]), func=ACT.Copy)
-        nc.vector.tensor_copy(out=k_sc[:], in_=scale_pool[:].bitcast(U8).indirect(k_list[:]))
-        gather_plane(2)
-        gather_plane(3)
-        nc.vector.quantize_mx(out=q_codes[:].bitcast(FP8X4), scales=q_scales[:],
+
+        nc.vector.tensor_copy(out=k_scale_picked[:], in_=scale_pool[:].bitcast(U8).indirect(k_list[:]))
+        for r in range(BLOCKS_PER_QUADRANT):
+            nc.sync.dma_start(out=k_scale_words[r:P:QUADRANT, :],
+                              in_=k_scale_picked[BLOCK_PARTITIONS * r:P:QUADRANT, :].bitcast(I32))
+
+        for t in VECTOR_PLANES:
+            nc.vector.tensor_copy(out=q_bf[:, :, t], in_=q_planes[t][:].indirect(q_list[:]))
+        nc.vector.quantize_mx(out=q_codes[:].bitcast(FP8X4), scales=q_scale_rows[:],
                               in_=q_bf[:].rearrange("p c t -> p (c t)"))
 
         scores = [psum.tile([P, N], F32, name=f"scores{b}") for b in range(B)]
         for b in range(B):
-            qc = slice(b * NQ, (b + 1) * NQ)
-            for h in range(N // PIECE):
-                c0 = b * N + h * PIECE
-                kc = slice(c0, c0 + PIECE)
-                nc.vector.tensor_copy(
-                    out=k_codes[:, kc],
-                    in_=word_pool[:].bitcast(U32).indirect(k_list[:, c0 // 16:(c0 + PIECE) // 16]))
+            queries = slice(b * NQ, (b + 1) * NQ)
+            for first in range(0, N, KEY_PIECE):
+                slots = slice(b * N + first, b * N + first + KEY_PIECE)
+                entries = k_list[:, slots.start // LIST_ROWS:slots.stop // LIST_ROWS]
+                nc.vector.tensor_copy(out=k_codes[:, slots], in_=word_pool[:].bitcast(U32).indirect(entries))
                 nc.tensor.matmul_mx(
-                    out=scores[b][:, h * PIECE:(h + 1) * PIECE],
-                    lhsT=q_codes[:, qc].bitcast(FP8X4), lhsT_scale=q_scales[:, qc],
-                    rhs=k_codes[:, kc].bitcast(FP8X4), rhs_scale=k_sc[:, kc],
+                    out=scores[b][:, first:first + KEY_PIECE],
+                    lhsT=q_codes[:, queries].bitcast(FP8X4), lhsT_scale=q_scale_rows[:, queries],
+                    rhs=k_codes[:, slots].bitcast(FP8X4), rhs_scale=k_scale_rows[:, slots],
                     start=True, stop=True)
 
         neg_max = [sb.tile([P, 1], F32, name=f"neg_max{b}") for b in range(B)]
         row_sum = [sb.tile([P, 1], F32, name=f"row_sum{b}") for b in range(B)]
         inv_sum = [sb.tile([P, 1], F32, name=f"inv_sum{b}") for b in range(B)]
-        expd = [sb.tile([P, N], F32, name=f"expd{b}") for b in range(B)]
-        res = [sb.tile([P, N], F32, name=f"res{b}") for b in range(B)]
+        exps = [sb.tile([P, N], F32, name=f"exps{b}") for b in range(B)]
+        weights = [sb.tile([P, N], F32, name=f"weights{b}") for b in range(B)]
         for b in range(B):
             nc.vector.tensor_reduce(out=neg_max[b][:], in_=scores[b][:], axis=AXIS.X, op=ALU.max, negate=True)
         for b in range(B):
-            nc.scalar.activation(out=expd[b][:], in_=scores[b][:], func=ACT.Exp,
+            nc.scalar.activation(out=exps[b][:], in_=scores[b][:], func=ACT.Exp,
                                  bias=neg_max[b][:], scale=1.0, accum_out=row_sum[b][:])
         for b in range(B):
             nc.vector.reciprocal(out=inv_sum[b][:], in_=row_sum[b][:])
-            for h in range(2):
-                cols = slice(h * N // 2, (h + 1) * N // 2)
-                nc.vector.tensor_scalar(out=res[b][:, cols], in0=expd[b][:, cols], scalar1=inv_sum[b][:],
+            for first in range(0, N, STORE_PIECE):
+                cols = slice(first, first + STORE_PIECE)
+                nc.vector.tensor_scalar(out=weights[b][:, cols], in0=exps[b][:, cols], scalar1=inv_sum[b][:],
                                         scalar2=None, op0=ALU.mult)
-                queue = nc.sync if h == 0 else nc.scalar
-                if b == 0:
-                    queue = nc.sync
-                queue.dma_start(out=out[b, :, cols], in_=res[b][:, cols])
+                is_last = b == B - 1 and cols.stop == N
+                queue = nc.scalar if is_last else nc.sync
+                queue.dma_start(out=out[b, :, cols], in_=weights[b][:, cols])

@@ -1,6 +1,7 @@
 from contextlib import ExitStack
 
 import concourse.mybir as mybir
+from concourse.masks import make_identity
 
 F32 = mybir.dt.float32
 BF16 = mybir.dt.bfloat16
@@ -76,6 +77,14 @@ def tile_attend_lq_wts_kernel(tc, qT, k_words, k_scales, offq, offs, out):
             nc.vector.tensor_copy(out=q_bf[:, :, t], in_=q_planes[t][:].indirect(q_list[:]))
         nc.vector.quantize_mx(out=q_codes[:].bitcast(FP8X4), scales=q_scale_rows[:],
                               in_=q_bf[:].rearrange("p c t -> p (c t)"))
+
+        identity = sb.tile([P, P], BF16, name="identity")
+        make_identity(nc, identity[:])
+        warm = psum.tile([P, PACK, P], BF16, name="warm")
+        q_flat = q_bf[:].rearrange("p c t -> p (c t)")
+        for source, count in ((q_cast[0][:], 14), (q_cast[1][:], 14), (q_flat, 4)):
+            for i in range(count):
+                nc.tensor.transpose(warm[:, i % PACK, :], source[:, (i % 8) * P:(i % 8 + 1) * P], identity[:])
 
         scores = [psum.tile([P, N], F32, name=f"scores{b}") for b in range(B)]
         for b in range(B):

@@ -1,7 +1,6 @@
 from contextlib import ExitStack
 
 import concourse.mybir as mybir
-from concourse.masks import make_identity
 
 F32 = mybir.dt.float32
 BF16 = mybir.dt.bfloat16
@@ -25,7 +24,8 @@ B, N, T, D, NQ, QPOOL = 2, 512, 2048, 512, 128, 1024
 KEY_PIECE = 256
 SCALAR_PLANES = (0, 1)
 VECTOR_PLANES = (2, 3)
-STORE_PIECE = N // 2
+FIRST_STORE = 128
+VECTOR_SHARE = 352
 
 FLOPS = 2 * B * NQ * N * D
 
@@ -78,14 +78,6 @@ def tile_attend_lq_wts_kernel(tc, qT, k_words, k_scales, offq, offs, out):
         nc.vector.quantize_mx(out=q_codes[:].bitcast(FP8X4), scales=q_scale_rows[:],
                               in_=q_bf[:].rearrange("p c t -> p (c t)"))
 
-        identity = sb.tile([P, P], BF16, name="identity")
-        make_identity(nc, identity[:])
-        warm = psum.tile([P, PACK, P], BF16, name="warm")
-        q_flat = q_bf[:].rearrange("p c t -> p (c t)")
-        for source, count in ((q_cast[0][:], 14), (q_cast[1][:], 14), (q_flat, 4)):
-            for i in range(count):
-                nc.tensor.transpose(warm[:, i % PACK, :], source[:, (i % 8) * P:(i % 8 + 1) * P], identity[:])
-
         scores = [psum.tile([P, N], F32, name=f"scores{b}") for b in range(B)]
         for b in range(B):
             queries = slice(b * NQ, (b + 1) * NQ)
@@ -109,12 +101,14 @@ def tile_attend_lq_wts_kernel(tc, qT, k_words, k_scales, offq, offs, out):
         for b in range(B):
             nc.scalar.activation(out=exps[b][:], in_=scores[b][:], func=ACT.Exp,
                                  bias=neg_max[b][:], scale=1.0, accum_out=row_sum[b][:])
-        for b in range(B):
-            nc.vector.reciprocal(out=inv_sum[b][:], in_=row_sum[b][:])
-            for first in range(0, N, STORE_PIECE):
-                cols = slice(first, first + STORE_PIECE)
-                nc.vector.tensor_scalar(out=weights[b][:, cols], in0=exps[b][:, cols], scalar1=inv_sum[b][:],
-                                        scalar2=None, op0=ALU.mult)
-                is_last = b == B - 1 and cols.stop == N
-                queue = nc.scalar if is_last else nc.sync
-                queue.dma_start(out=out[b, :, cols], in_=weights[b][:, cols])
+        nc.vector.reciprocal(out=inv_sum[0][:], in_=row_sum[0][:])
+        for cols in (slice(0, FIRST_STORE), slice(FIRST_STORE, N)):
+            nc.vector.tensor_scalar(out=weights[0][:, cols], in0=exps[0][:, cols], scalar1=inv_sum[0][:],
+                                    scalar2=None, op0=ALU.mult)
+            nc.sync.dma_start(out=out[0, :, cols], in_=weights[0][:, cols])
+        nc.vector.reciprocal(out=inv_sum[1][:], in_=row_sum[1][:])
+        nc.vector.tensor_scalar(out=weights[1][:, :VECTOR_SHARE], in0=exps[1][:, :VECTOR_SHARE],
+                                scalar1=inv_sum[1][:], scalar2=None, op0=ALU.mult)
+        nc.scalar.activation(out=weights[1][:, VECTOR_SHARE:], in_=exps[1][:, VECTOR_SHARE:], func=ACT.Copy,
+                             scale=inv_sum[1][:])
+        nc.sync.dma_start(out=out[1], in_=weights[1][:])

@@ -23,7 +23,7 @@ B, N, T, D, NQ, QPOOL = 2, 512, 2048, 512, 128, 1024
 
 KEY_PIECE = 256
 SCALAR_PLANES = (0, 1)
-VECTOR_PLANES = (2, 3)
+WARM_PASSES, WARM_ROWS = 8, 32
 FIRST_STORE = 128
 VECTOR_SHARE = 352
 
@@ -65,18 +65,32 @@ def tile_attend_lq_wts_kernel(tc, qT, k_words, k_scales, offq, offs, out):
         q_cast = [sb.tile([P, QPOOL], BF16, name=f"q_cast{t}") for t in SCALAR_PLANES]
         for t in SCALAR_PLANES:
             nc.scalar.copy(out=q_cast[t][:], in_=q_planes[t][:])
-        for t in SCALAR_PLANES:
-            nc.scalar.activation(out=q_bf[:, :, t], in_=q_cast[t][:].indirect(q_list[:]), func=ACT.Copy)
+        by_sequence = [slice(b * NQ, (b + 1) * NQ) for b in range(B)]
+        q_entries = [q_list[:, q.start // LIST_ROWS:q.stop // LIST_ROWS] for q in by_sequence]
+        nc.scalar.activation(out=q_bf[:, :, 0], in_=q_cast[0][:].indirect(q_list[:]), func=ACT.Copy)
+        for queries, entries in zip(by_sequence, q_entries):
+            nc.scalar.activation(out=q_bf[:, queries, 1], in_=q_cast[1][:].indirect(entries), func=ACT.Copy)
 
         nc.vector.tensor_copy(out=k_scale_picked[:], in_=scale_pool[:].bitcast(U8).indirect(k_list[:]))
         for r in range(BLOCKS_PER_QUADRANT):
             nc.sync.dma_start(out=k_scale_words[r:P:QUADRANT, :],
                               in_=k_scale_picked[BLOCK_PARTITIONS * r:P:QUADRANT, :].bitcast(I32))
 
-        for t in VECTOR_PLANES:
-            nc.vector.tensor_copy(out=q_bf[:, :, t], in_=q_planes[t][:].indirect(q_list[:]))
-        nc.vector.quantize_mx(out=q_codes[:].bitcast(FP8X4), scales=q_scale_rows[:],
-                              in_=q_bf[:].rearrange("p c t -> p (c t)"))
+        nc.vector.tensor_copy(out=q_bf[:, :, 2], in_=q_planes[2][:].indirect(q_list[:]))
+        for queries, entries in zip(by_sequence, q_entries):
+            nc.vector.tensor_copy(out=q_bf[:, queries, 3], in_=q_planes[3][:].indirect(entries))
+        for queries in by_sequence:
+            nc.vector.quantize_mx(out=q_codes[:, queries].bitcast(FP8X4), scales=q_scale_rows[:, queries],
+                                  in_=q_bf[:, queries, :].rearrange("p c t -> p (c t)"))
+
+        idle = [psum.tile([P, N], F32, name=f"idle{j}") for j in range(WARM_PASSES * NQ // N)]
+        for j in range(WARM_PASSES):
+            first = j * NQ % N
+            nc.tensor.matmul_mx(
+                out=idle[j * NQ // N][0:WARM_ROWS, first:first + NQ],
+                lhsT=q_codes[:, 0:WARM_ROWS].bitcast(FP8X4), lhsT_scale=q_scale_rows[:, 0:WARM_ROWS],
+                rhs=q_codes[:, 0:NQ].bitcast(FP8X4), rhs_scale=q_scale_rows[:, 0:NQ],
+                start=True, stop=True)
 
         scores = [psum.tile([P, N], F32, name=f"scores{b}") for b in range(B)]
         for b in range(B):

@@ -23,7 +23,6 @@ B, N, T, D, NQ, QPOOL = 2, 512, 2048, 512, 128, 1024
 
 KEY_PIECE = 256
 SCALAR_PLANES = (0, 1)
-WARM_PASSES, WARM_ROWS = 8, 32
 FIRST_STORE = 128
 VECTOR_SHARE = 352
 
@@ -82,15 +81,6 @@ def tile_attend_lq_wts_kernel(tc, qT, k_words, k_scales, offq, offs, out):
         for queries in by_sequence:
             nc.vector.quantize_mx(out=q_codes[:, queries].bitcast(FP8X4), scales=q_scale_rows[:, queries],
                                   in_=q_bf[:, queries, :].rearrange("p c t -> p (c t)"))
-
-        idle = [psum.tile([P, N], F32, name=f"idle{j}") for j in range(WARM_PASSES * NQ // N)]
-        for j in range(WARM_PASSES):
-            first = j * NQ % N
-            nc.tensor.matmul_mx(
-                out=idle[j * NQ // N][0:WARM_ROWS, first:first + NQ],
-                lhsT=q_codes[:, 0:WARM_ROWS].bitcast(FP8X4), lhsT_scale=q_scale_rows[:, 0:WARM_ROWS],
-                rhs=q_codes[:, 0:NQ].bitcast(FP8X4), rhs_scale=q_scale_rows[:, 0:NQ],
-                start=True, stop=True)
 
         scores = [psum.tile([P, N], F32, name=f"scores{b}") for b in range(B)]
         for b in range(B):

@@ -25,6 +25,7 @@ KEY_PIECE = 256
 SCALAR_PLANES = (0, 1)
 FIRST_STORE = 128
 VECTOR_SHARE = 352
+DMA_ALIGN = 256
 
 FLOPS = 2 * B * NQ * N * D
 
@@ -38,9 +39,9 @@ def tile_attend_lq_wts_kernel(tc, qT, k_words, k_scales, offq, offs, out):
 
         q_list = lists.tile([P, B * NQ // LIST_ROWS], U16, name="q_list")
         k_list = lists.tile([P, B * N // LIST_ROWS], U16, name="k_list")
-        q_planes = [sb.tile([P, QPOOL], F32, name=f"q_plane{t}") for t in range(PACK)]
-        word_pool = sb.tile([P, T], I32, name="word_pool")
-        scale_pool = sb.tile([P, T // 4], I32, name="scale_pool")
+        q_planes = [sb.tile([P, QPOOL], F32, name=f"q_plane{t}", align_bytes=DMA_ALIGN) for t in range(PACK)]
+        word_pool = sb.tile([P, T], I32, name="word_pool", align_bytes=DMA_ALIGN)
+        scale_pool = sb.tile([P, T // 4], I32, name="scale_pool", align_bytes=DMA_ALIGN)
 
         nc.vector.memset(scale_pool[:], 0)
 
@@ -57,8 +58,8 @@ def tile_attend_lq_wts_kernel(tc, qT, k_words, k_scales, offq, offs, out):
         q_codes = sb.tile([P, B * NQ], U32, name="q_codes", align_bytes=64)
         q_scale_rows = sb.tile([P, B * NQ], U8, name="q_scale_rows", align_bytes=64)
         k_codes = sb.tile([P, B * N], U32, name="k_codes", align_bytes=64)
-        k_scale_picked = sb.tile([P, B * N], U8, name="k_scale_picked", align_bytes=64)
-        k_scale_words = sb.tile([P, B * N // 4], I32, name="k_scale_words", align_bytes=64)
+        k_scale_picked = sb.tile([P, B * N], U8, name="k_scale_picked", align_bytes=DMA_ALIGN)
+        k_scale_words = sb.tile([P, B * N // 4], I32, name="k_scale_words", align_bytes=DMA_ALIGN)
         k_scale_rows = k_scale_words[:].bitcast(U8)
 
         q_cast = [sb.tile([P, QPOOL], BF16, name=f"q_cast{t}") for t in SCALAR_PLANES]
@@ -99,7 +100,7 @@ def tile_attend_lq_wts_kernel(tc, qT, k_words, k_scales, offq, offs, out):
         row_sum = [sb.tile([P, 1], F32, name=f"row_sum{b}") for b in range(B)]
         inv_sum = [sb.tile([P, 1], F32, name=f"inv_sum{b}") for b in range(B)]
         exps = [sb.tile([P, N], F32, name=f"exps{b}") for b in range(B)]
-        weights = [sb.tile([P, N], F32, name=f"weights{b}") for b in range(B)]
+        weights = [sb.tile([P, N], F32, name=f"weights{b}", align_bytes=DMA_ALIGN) for b in range(B)]
         for b in range(B):
             nc.vector.tensor_reduce(out=neg_max[b][:], in_=scores[b][:], axis=AXIS.X, op=ALU.max, negate=True)
         for b in range(B):

@@ -25,7 +25,7 @@ KEY_PIECE = 256
 SCALAR_PLANES = (0, 1)
 FIRST_STORE = 128
 VECTOR_SHARE = 352
-DMA_ALIGN = 256
+DMA_ALIGN = 4096
 
 FLOPS = 2 * B * NQ * N * D
 
@@ -37,8 +37,8 @@ def tile_attend_lq_wts_kernel(tc, qT, k_words, k_scales, offq, offs, out):
         sb = ctx.enter_context(tc.tile_pool(name="sb", bufs=1))
         psum = ctx.enter_context(tc.psum_pool(name="psum", bufs=1))
 
-        q_list = lists.tile([P, B * NQ // LIST_ROWS], U16, name="q_list")
-        k_list = lists.tile([P, B * N // LIST_ROWS], U16, name="k_list")
+        q_list = lists.tile([P, B * NQ // LIST_ROWS], U16, name="q_list", align_bytes=256)
+        k_list = lists.tile([P, B * N // LIST_ROWS], U16, name="k_list", align_bytes=256)
         q_planes = [sb.tile([P, QPOOL], F32, name=f"q_plane{t}", align_bytes=DMA_ALIGN) for t in range(PACK)]
         word_pool = sb.tile([P, T], I32, name="word_pool", align_bytes=DMA_ALIGN)
         scale_pool = sb.tile([P, T // 4], I32, name="scale_pool", align_bytes=DMA_ALIGN)

@@ -47,9 +47,9 @@ def tile_attend_lq_wts_kernel(tc, qT, k_words, k_scales, offq, offs, out):
 
         q_rows = qT.rearrange("(p t) c -> p t c", t=PACK)
         nc.sync.dma_start(out=q_planes[0][:], in_=q_rows[:, 0, :])
-        nc.sync.dma_start(q_list[:], offq)
         nc.sync.dma_start(k_list[:], offs)
         nc.sync.dma_start(out=scale_pool[0:P:BLOCK_PARTITIONS, :], in_=k_scales[0].bitcast(I32))
+        nc.sync.dma_start(q_list[:], offq)
         for t in range(1, PACK):
             nc.sync.dma_start(out=q_planes[t][:], in_=q_rows[:, t, :])
         nc.sync.dma_start(out=word_pool[:], in_=k_words[0].rearrange("p n t -> p (n t)").bitcast(I32))
@@ -72,9 +72,13 @@ def tile_attend_lq_wts_kernel(tc, qT, k_words, k_scales, offq, offs, out):
             nc.scalar.activation(out=q_bf[:, queries, 1], in_=q_cast[1][:].indirect(entries), func=ACT.Copy)
 
         nc.vector.tensor_copy(out=k_scale_picked[:], in_=scale_pool[:].bitcast(U8).indirect(k_list[:]))
-        for r in range(BLOCKS_PER_QUADRANT):
-            nc.sync.dma_start(out=k_scale_words[r:P:QUADRANT, :],
-                              in_=k_scale_picked[BLOCK_PARTITIONS * r:P:QUADRANT, :].bitcast(I32))
+        picked_words = k_scale_picked[:].bitcast(I32)
+        nc.vector.tensor_copy(out=k_scale_words[:], in_=picked_words)
+        whole, half = slice(0, B * N // 4), N // 4
+        first, second = slice(0, half), slice(half, 2 * half)
+        for r, cols in ((1, whole), (2, first), (3, first), (2, second), (3, second)):
+            nc.sync.dma_start(out=k_scale_words[r:P:QUADRANT, cols],
+                              in_=picked_words[BLOCK_PARTITIONS * r:P:QUADRANT, cols])
 
         nc.vector.tensor_copy(out=q_bf[:, :, 2], in_=q_planes[2][:].indirect(q_list[:]))
         for queries, entries in zip(by_sequence, q_entries):

@@ -22,7 +22,9 @@ BLOCK_PARTITIONS = 8
 B, N, T, D, NQ, QPOOL = 2, 512, 2048, 512, 128, 1024
 
 KEY_PIECE = 256
-SCALAR_PLANES = (0, 1)
+SCALAR_PICKS = ((0, 0), (0, 1), (3, 0), (2, 1), (3, 1))
+VECTOR_PICKS = ((1, 0), (2, 0), (1, 1))
+LINE_WORDS = 4
 FIRST_STORE = 128
 VECTOR_SHARE = 352
 DMA_ALIGN = 4096
@@ -39,22 +41,27 @@ def tile_attend_lq_wts_kernel(tc, qT, k_words, k_scales, offq, offs, out):
 
         q_list = lists.tile([P, B * NQ // LIST_ROWS], U16, name="q_list", align_bytes=256)
         k_list = lists.tile([P, B * N // LIST_ROWS], U16, name="k_list", align_bytes=256)
-        q_planes = [sb.tile([P, QPOOL], F32, name=f"q_plane{t}", align_bytes=DMA_ALIGN) for t in range(PACK)]
+        q_first = sb.tile([P, QPOOL], F32, name="q_first", align_bytes=DMA_ALIGN)
+        q_rest = sb.tile([P, 3 * QPOOL], F32, name="q_rest", align_bytes=DMA_ALIGN)
+        q_planes = [q_first[:]] + [q_rest[:, u * QPOOL:(u + 1) * QPOOL] for u in range(PACK - 1)]
         word_pool = sb.tile([P, T], I32, name="word_pool", align_bytes=DMA_ALIGN)
         scale_pool = sb.tile([P, T // 4], I32, name="scale_pool", align_bytes=DMA_ALIGN)
 
         nc.vector.memset(scale_pool[:], 0)
 
-        q_rows = qT.rearrange("(p t) c -> p t c", t=PACK)
-        nc.sync.dma_start(out=q_planes[0][:], in_=q_rows[:, 0, :])
+        idle = lists.tile([P, 2], F32, name="idle")
+        nc.gpsimd.memset(idle[:, 0:1], 0.0)
+        nc.scalar.activation(out=idle[:, 1:2], in_=idle[:, 0:1], func=ACT.Exp)
+
+        q_rows = qT.rearrange("(p t) c -> p (t c)", t=PACK)
+        nc.sync.dma_start(out=q_first[:], in_=q_rows[:, :QPOOL])
         nc.sync.dma_start(k_list[:], offs)
-        nc.sync.dma_start(out=scale_pool[0:P:BLOCK_PARTITIONS, :], in_=k_scales[0].bitcast(I32))
         nc.sync.dma_start(q_list[:], offq)
-        for t in range(1, PACK):
-            nc.sync.dma_start(out=q_planes[t][:], in_=q_rows[:, t, :])
+        nc.sync.dma_start(out=scale_pool[0:P:BLOCK_PARTITIONS, :], in_=k_scales[0].bitcast(I32))
+        nc.sync.dma_start(out=q_rest[:], in_=q_rows[:, QPOOL:])
         nc.sync.dma_start(out=word_pool[:], in_=k_words[0].rearrange("p n t -> p (n t)").bitcast(I32))
 
-        q_bf = sb.tile([P, B * NQ, PACK], BF16, name="q_bf", align_bytes=64)
+        q_bf = [sb.tile([P, NQ, PACK], BF16, name=f"q_bf{b}", align_bytes=64) for b in range(B)]
         q_codes = sb.tile([P, B * NQ], U32, name="q_codes", align_bytes=64)
         q_scale_rows = sb.tile([P, B * NQ], U8, name="q_scale_rows", align_bytes=64)
         k_codes = sb.tile([P, B * N], U32, name="k_codes", align_bytes=64)
@@ -62,30 +69,29 @@ def tile_attend_lq_wts_kernel(tc, qT, k_words, k_scales, offq, offs, out):
         k_scale_words = sb.tile([P, B * N // 4], I32, name="k_scale_words", align_bytes=DMA_ALIGN)
         k_scale_rows = k_scale_words[:].bitcast(U8)
 
-        q_cast = [sb.tile([P, QPOOL], BF16, name=f"q_cast{t}") for t in SCALAR_PLANES]
-        for t in SCALAR_PLANES:
-            nc.scalar.copy(out=q_cast[t][:], in_=q_planes[t][:])
         by_sequence = [slice(b * NQ, (b + 1) * NQ) for b in range(B)]
         q_entries = [q_list[:, q.start // LIST_ROWS:q.stop // LIST_ROWS] for q in by_sequence]
-        nc.scalar.activation(out=q_bf[:, :, 0], in_=q_cast[0][:].indirect(q_list[:]), func=ACT.Copy)
-        for queries, entries in zip(by_sequence, q_entries):
-            nc.scalar.activation(out=q_bf[:, queries, 1], in_=q_cast[1][:].indirect(entries), func=ACT.Copy)
+        q_picked = [sb.tile([P, PACK, NQ], F32, name=f"q_picked{b}", align_bytes=64) for b in range(B)]
+        for t, b in SCALAR_PICKS:
+            nc.scalar.activation(out=q_picked[b][:, t, :], in_=q_planes[t].indirect(q_entries[b]), func=ACT.Copy)
 
         nc.vector.tensor_copy(out=k_scale_picked[:], in_=scale_pool[:].bitcast(U8).indirect(k_list[:]))
         picked_words = k_scale_picked[:].bitcast(I32)
         nc.vector.tensor_copy(out=k_scale_words[:], in_=picked_words)
-        whole, half = slice(0, B * N // 4), N // 4
-        first, second = slice(0, half), slice(half, 2 * half)
-        for r, cols in ((1, whole), (2, first), (3, first), (2, second), (3, second)):
+        piece = KEY_PIECE // 4
+        stretches = (slice(0, piece), slice(piece, 2 * piece), slice(2 * piece, 4 * piece))
+        for r, cols in [(1, slice(0, 4 * piece))] + [(r, cols) for cols in stretches for r in (2, 3)]:
             nc.sync.dma_start(out=k_scale_words[r:P:QUADRANT, cols],
                               in_=picked_words[BLOCK_PARTITIONS * r:P:QUADRANT, cols])
 
-        nc.vector.tensor_copy(out=q_bf[:, :, 2], in_=q_planes[2][:].indirect(q_list[:]))
-        for queries, entries in zip(by_sequence, q_entries):
-            nc.vector.tensor_copy(out=q_bf[:, queries, 3], in_=q_planes[3][:].indirect(entries))
-        for queries in by_sequence:
+        for t, b in VECTOR_PICKS:
+            nc.vector.tensor_copy(out=q_picked[b][:, t, :], in_=q_planes[t].indirect(q_entries[b]))
+        for b in range(B):
+            nc.vector.tensor_copy(out=q_bf[b][:].rearrange("p (c i) t -> p c t i", i=LINE_WORDS),
+                                  in_=q_picked[b][:].rearrange("p t (c i) -> p c t i", i=LINE_WORDS))
+        for b, queries in enumerate(by_sequence):
             nc.vector.quantize_mx(out=q_codes[:, queries].bitcast(FP8X4), scales=q_scale_rows[:, queries],
-                                  in_=q_bf[:, queries, :].rearrange("p c t -> p (c t)"))
+                                  in_=q_bf[b][:].rearrange("p c t -> p (c t)"))
 
         scores = [psum.tile([P, N], F32, name=f"scores{b}") for b in range(B)]
         for b in range(B):

from contextlib import ExitStack

import concourse.mybir as mybir

F32 = mybir.dt.float32
BF16 = mybir.dt.bfloat16
I32 = mybir.dt.int32
U32 = mybir.dt.uint32
U16 = mybir.dt.uint16
U8 = mybir.dt.uint8
FP8X4 = mybir.dt.float8_e4m3fn_x4
ALU = mybir.AluOpType
ACT = mybir.ActivationFunctionType
AXIS = mybir.AxisListType

P = 128
PACK = 4
LIST_ROWS = 16
QUADRANT = 32
BLOCKS_PER_QUADRANT = 4
BLOCK_PARTITIONS = 8
B, N, T, D, NQ, QPOOL = 2, 512, 2048, 512, 128, 1024

KEY_PIECE = 256
SCALAR_PICKS = ((0, 0), (0, 1), (3, 0), (2, 1), (3, 1))
VECTOR_PICKS = ((1, 0), (2, 0), (1, 1))
LINE_WORDS = 4
FIRST_STORE = 128
VECTOR_SHARE = 352
DMA_ALIGN = 4096

FLOPS = 2 * B * NQ * N * D


def tile_attend_lq_wts_kernel(tc, qT, k_words, k_scales, offq, offs, out):
    nc = tc.nc
    with ExitStack() as ctx:
        lists = ctx.enter_context(tc.tile_pool(name="lists", bufs=1))
        sb = ctx.enter_context(tc.tile_pool(name="sb", bufs=1))
        psum = ctx.enter_context(tc.psum_pool(name="psum", bufs=1))

        q_list = lists.tile([P, B * NQ // LIST_ROWS], U16, name="q_list", align_bytes=256)
        k_list = lists.tile([P, B * N // LIST_ROWS], U16, name="k_list", align_bytes=256)
        q_first = sb.tile([P, QPOOL], F32, name="q_first", align_bytes=DMA_ALIGN)
        q_rest = sb.tile([P, 3 * QPOOL], F32, name="q_rest", align_bytes=DMA_ALIGN)
        q_planes = [q_first[:]] + [q_rest[:, u * QPOOL:(u + 1) * QPOOL] for u in range(PACK - 1)]
        word_pool = sb.tile([P, T], I32, name="word_pool", align_bytes=DMA_ALIGN)
        scale_pool = sb.tile([P, T // 4], I32, name="scale_pool", align_bytes=DMA_ALIGN)

        nc.vector.memset(scale_pool[:], 0)

        idle = lists.tile([P, 2], F32, name="idle")
        nc.gpsimd.memset(idle[:, 0:1], 0.0)
        nc.scalar.activation(out=idle[:, 1:2], in_=idle[:, 0:1], func=ACT.Exp)

        q_rows = qT.rearrange("(p t) c -> p (t c)", t=PACK)
        nc.sync.dma_start(out=q_first[:], in_=q_rows[:, :QPOOL])
        nc.sync.dma_start(k_list[:], offs)
        nc.sync.dma_start(q_list[:], offq)
        nc.sync.dma_start(out=scale_pool[0:P:BLOCK_PARTITIONS, :], in_=k_scales[0].bitcast(I32))
        nc.sync.dma_start(out=q_rest[:], in_=q_rows[:, QPOOL:])
        nc.sync.dma_start(out=word_pool[:], in_=k_words[0].rearrange("p n t -> p (n t)").bitcast(I32))

        q_bf = [sb.tile([P, NQ, PACK], BF16, name=f"q_bf{b}", align_bytes=64) for b in range(B)]
        q_codes = sb.tile([P, B * NQ], U32, name="q_codes", align_bytes=64)
        q_scale_rows = sb.tile([P, B * NQ], U8, name="q_scale_rows", align_bytes=64)
        k_codes = sb.tile([P, B * N], U32, name="k_codes", align_bytes=64)
        k_scale_picked = sb.tile([P, B * N], U8, name="k_scale_picked", align_bytes=DMA_ALIGN)
        k_scale_words = sb.tile([P, B * N // 4], I32, name="k_scale_words", align_bytes=DMA_ALIGN)
        k_scale_rows = k_scale_words[:].bitcast(U8)

        by_sequence = [slice(b * NQ, (b + 1) * NQ) for b in range(B)]
        q_entries = [q_list[:, q.start // LIST_ROWS:q.stop // LIST_ROWS] for q in by_sequence]
        q_picked = [sb.tile([P, PACK, NQ], F32, name=f"q_picked{b}", align_bytes=64) for b in range(B)]
        for t, b in SCALAR_PICKS:
            nc.scalar.activation(out=q_picked[b][:, t, :], in_=q_planes[t].indirect(q_entries[b]), func=ACT.Copy)

        nc.vector.tensor_copy(out=k_scale_picked[:], in_=scale_pool[:].bitcast(U8).indirect(k_list[:]))
        picked_words = k_scale_picked[:].bitcast(I32)
        nc.vector.tensor_copy(out=k_scale_words[:], in_=picked_words)
        piece = KEY_PIECE // 4
        stretches = (slice(0, piece), slice(piece, 2 * piece), slice(2 * piece, 4 * piece))
        for r, cols in [(1, slice(0, 4 * piece))] + [(r, cols) for cols in stretches for r in (2, 3)]:
            nc.sync.dma_start(out=k_scale_words[r:P:QUADRANT, cols],
                              in_=picked_words[BLOCK_PARTITIONS * r:P:QUADRANT, cols])

        for t, b in VECTOR_PICKS:
            nc.vector.tensor_copy(out=q_picked[b][:, t, :], in_=q_planes[t].indirect(q_entries[b]))
        for b in range(B):
            nc.vector.tensor_copy(out=q_bf[b][:].rearrange("p (c i) t -> p c t i", i=LINE_WORDS),
                                  in_=q_picked[b][:].rearrange("p t (c i) -> p c t i", i=LINE_WORDS))
        for b, queries in enumerate(by_sequence):
            nc.vector.quantize_mx(out=q_codes[:, queries].bitcast(FP8X4), scales=q_scale_rows[:, queries],
                                  in_=q_bf[b][:].rearrange("p c t -> p (c t)"))

        scores = [psum.tile([P, N], F32, name=f"scores{b}") for b in range(B)]
        for b in range(B):
            queries = slice(b * NQ, (b + 1) * NQ)
            for first in range(0, N, KEY_PIECE):
                slots = slice(b * N + first, b * N + first + KEY_PIECE)
                entries = k_list[:, slots.start // LIST_ROWS:slots.stop // LIST_ROWS]
                nc.vector.tensor_copy(out=k_codes[:, slots], in_=word_pool[:].bitcast(U32).indirect(entries))
                nc.tensor.matmul_mx(
                    out=scores[b][:, first:first + KEY_PIECE],
                    lhsT=q_codes[:, queries].bitcast(FP8X4), lhsT_scale=q_scale_rows[:, queries],
                    rhs=k_codes[:, slots].bitcast(FP8X4), rhs_scale=k_scale_rows[:, slots],
                    start=True, stop=True)

        neg_max = [sb.tile([P, 1], F32, name=f"neg_max{b}") for b in range(B)]
        row_sum = [sb.tile([P, 1], F32, name=f"row_sum{b}") for b in range(B)]
        inv_sum = [sb.tile([P, 1], F32, name=f"inv_sum{b}") for b in range(B)]
        exps = [sb.tile([P, N], F32, name=f"exps{b}") for b in range(B)]
        weights = [sb.tile([P, N], F32, name=f"weights{b}", align_bytes=DMA_ALIGN) for b in range(B)]
        for b in range(B):
            nc.vector.tensor_reduce(out=neg_max[b][:], in_=scores[b][:], axis=AXIS.X, op=ALU.max, negate=True)
        for b in range(B):
            nc.scalar.activation(out=exps[b][:], in_=scores[b][:], func=ACT.Exp,
                                 bias=neg_max[b][:], scale=1.0, accum_out=row_sum[b][:])
        nc.vector.reciprocal(out=inv_sum[0][:], in_=row_sum[0][:])
        for cols in (slice(0, FIRST_STORE), slice(FIRST_STORE, N)):
            nc.vector.tensor_scalar(out=weights[0][:, cols], in0=exps[0][:, cols], scalar1=inv_sum[0][:],
                                    scalar2=None, op0=ALU.mult)
            nc.sync.dma_start(out=out[0, :, cols], in_=weights[0][:, cols])
        nc.vector.reciprocal(out=inv_sum[1][:], in_=row_sum[1][:])
        nc.vector.tensor_scalar(out=weights[1][:, :VECTOR_SHARE], in0=exps[1][:, :VECTOR_SHARE],
                                scalar1=inv_sum[1][:], scalar2=None, op0=ALU.mult)
        nc.scalar.activation(out=weights[1][:, VECTOR_SHARE:], in_=exps[1][:, VECTOR_SHARE:], func=ACT.Copy,
                             scale=inv_sum[1][:])
        nc.sync.dma_start(out=out[1], in_=weights[1][:])
